import numpy as np, ml_dtypes
CORES = [2,3,42,43,82,83,122,123]
N = 8
import mx_ref
BF = ml_dtypes.bfloat16
def entries(a):
    return np.ascontiguousarray(a.T).reshape(-1)
def table(e):
    return np.ascontiguousarray(np.reshape(e, (-1, 16)).T).astype(np.int32)
def cols(t, e):
    v = np.concatenate([t.reshape(128, -1, 4), np.zeros((128, 1, 4), BF)], axis=1)
    return np.ascontiguousarray(v[:, e]).reshape(128, -1)
def f(rng, *shape):
    return mx_ref.flush((rng.standard_normal(shape, dtype=np.float32) * np.exp2(rng.integers(-2, 3, shape[:-1] + (1,)))).astype(BF))
def wide(rng, *shape, cols=0):
    v = rng.standard_normal(shape, dtype=np.float32) * np.exp2(rng.integers(-12, 13, shape)).astype(np.float32)
    if cols: v *= np.repeat(np.exp2(rng.integers(-cols, cols + 1, shape[:-2] + (1, shape[-1] // 4))) * (rng.random(shape[:-2] + (1, shape[-1] // 4)) > 0.0625), 4, axis=-1).astype(np.float32)
    return mx_ref.flush(v.astype(BF))
T, NA, S, CAPP = 1024, 512, 512, 96
def lists(rng, most=0, inorder=False, big=None):
    c, m = [], []
    for r in range(N):
        n = np.zeros(N, int)
        n[rng.permutation(N)[:most]] = CAPP
        while n.sum() < S:
            q = rng.integers(0, N)
            if n[q] < CAPP: n[q] += 1
        used = np.concatenate([q * CAPP + rng.permutation(CAPP)[:n[q]] for q in range(N)])
        slots = np.full(N * CAPP, -1); slots[used] = rng.integers(0, T, S)
        o = np.sort(used) if inorder else rng.permutation(used)
        if big is not None:
            for i in range(S // 32):
                k = o[32 * i + rng.integers(0, 32)]; slots[k] = rng.choice(big[k // CAPP])
        c.append(table(slots)); m.append(table(o))
    return {"want": np.stack(c), "slot": np.stack(m)}
def setup_inputs(rng):
    return {"v": f(rng, N, 128, 4 * T), "a": f(rng, N, 128, 4 * NA), **lists(rng)}
def setup_inputs_full(rng):
    return {**setup_inputs(rng), **lists(rng, most=S // CAPP)}
def setup_inputs_sorted(rng):
    return {**setup_inputs(rng), **lists(rng, inorder=True)}
def setup_inputs_giant(rng):
    d = setup_inputs(rng); big = [rng.permutation(T)[:T // 32] for q in range(N)]
    x = d["v"].reshape(N, 128, T, 4)
    for q in range(N): x[q][:, big[q]] = (x[q][:, big[q]].astype(np.float32) * np.float32(2.0 ** 20)).astype(BF)
    d["v"] = x.reshape(N, 128, 4 * T)
    return {**d, **lists(rng, big=big)}
def setup_inputs_spread(rng):
    d = setup_inputs(rng); d["v"] = wide(rng, N, 128, 4 * T); d["a"] = wide(rng, N, 128, 4 * NA); return d
def check_inputs(d):
    b = []
    for r in range(N):
        c, m = entries(d["want"][r]), entries(d["slot"][r])
        if c.min() < -1 or c.max() >= T or (c >= 0).sum() != S: b.append("want")
        if m.min() < 0 or m.max() >= N * CAPP or len(set(m.tolist())) != S or (c[np.clip(m, 0, N * CAPP - 1)] < 0).any(): b.append("slot")
    return b
def ones(b):
    e = np.zeros((128, 128, 4), np.float32); e[np.arange(128), np.arange(128), b] = 1
    return e.reshape(128, 512).astype(BF)
def decode(q):
    return np.stack([mx_ref.matmul(mx_ref.quantize(ones(b)), q) for b in range(4)], axis=1).reshape(512, -1)
def reference(v, a, want, slot, own=None):
    h = np.zeros((N, 128, 2048), BF); y = np.zeros((N, 128, 4 * NA), np.float32)
    for r in range(N):
        c = entries(want[r])
        arrived = np.concatenate([decode(mx_ref.quantize(cols(v[q], c[q * CAPP:(q + 1) * CAPP]))) for q in range(N)], axis=1)
        H = arrived[:, entries(slot[r])].T
        h[r] = H.reshape(128, 4, 512).transpose(0, 2, 1).reshape(128, 2048).astype(BF)
    for r in range(N):
        t = h[r] if own is None else np.asarray(own["h"][r])
        for o in range(4):
            y[r][:, NA * o:NA * o + NA] = mx_ref.matmul(mx_ref.quantize(np.ascontiguousarray(t[:, 512 * o:512 * o + 512])), mx_ref.quantize(a[r]))
    return {"y": y, "h": h}

@@ -1,0 +1,268 @@
+from concourse.bass import DstId, RemoteDMATransfer
+from concourse.mybir import dt, AluOpType, ActivationFunctionType
+
+N, CAPP = 8, 96
+L = CAPP // 16
+P2 = 2 * CAPP
+E4 = "float8_e4m3fn_x4"
+
+SCRATCH = {
+    "wraw": ("sbuf", [128, N * L], "int32"), "wl": ("sbuf", [128, N * L], "uint16"),
+    "sraw": ("sbuf", [128, 32], "int32"), "sn": ("sbuf", [128, 32], "uint16"), "so": ("sbuf", [128, 32], "uint16"),
+    "sx": ("sbuf", [128, 64], "float32"), "st": ("sbuf", [128, 64], "float32"),
+    "l0": ("sbuf", [128, 2 * L], "uint16"), "l1": ("sbuf", [128, 3 * L], "uint16"), "l2": ("sbuf", [128, 2 * L], "uint16"),
+    "vt": ("sbuf", [128, 4096], "bfloat16"), "at": ("sbuf", [128, 2048], "bfloat16"),
+    "t0": ("sbuf", [128, 4 * P2], "bfloat16"), "t1": ("sbuf", [128, 4 * (P2 + CAPP)], "bfloat16"), "t2": ("sbuf", [128, 4 * P2], "bfloat16"),
+    "q0": ("sbuf", [128, P2], E4), "x0": ("sbuf", [128, P2], "uint8"),
+    "q1": ("sbuf", [128, P2 + CAPP], E4), "x1": ("sbuf", [128, P2 + CAPP], "uint8"),
+    "q2": ("sbuf", [128, P2], E4), "x2": ("sbuf", [128, P2], "uint8"),
+    "town": ("sbuf", [128, 512], "bfloat16"),
+    "r0": ("sbuf", [128, P2], E4), "rx0": ("sbuf", [128, P2], "uint8"),
+    "r1": ("sbuf", [128, P2], E4), "rx1": ("sbuf", [128, P2], "uint8"),
+    "r2": ("sbuf", [128, P2], E4), "rx2": ("sbuf", [128, P2], "uint8"),
+    "rn": ("sbuf", [128, 224], E4), "rxn": ("sbuf", [128, 224], "uint8"),
+    "qm": ("sbuf", [128, 512], E4), "xm": ("sbuf", [128, 512], "uint8"),
+    "kk": ("sbuf", [128, 512], "bfloat16"), "kc": ("sbuf", [128, 2], "float32"), "kb": ("sbuf", [128, 8], "float32"),
+    "kd": ("sbuf", [128, 128], "float32"), "idn": ("sbuf", [128, 128], "float32"),
+    "et": ("sbuf", [128, 2048], "bfloat16"), "qe": ("sbuf", [128, 512], E4), "xe": ("sbuf", [128, 512], "uint8"),
+    "win": ("sbuf", [128, 4 * N * CAPP], "bfloat16"),
+    "gf": ("sbuf", [128, 1024], "float32"), "gb": ("sbuf", [128, 1024], "bfloat16"), "tr": ("sbuf", [128, 1024], "bfloat16"),
+    "ht": ("sbuf", [128, 2048], "bfloat16"), "qh": ("sbuf", [128, 512], E4), "xh": ("sbuf", [128, 512], "uint8"),
+    "yt": ("sbuf", [128, 2048], "float32"),
+    "p0": ("psum", [128, 2048], "float32"), "p1": ("psum", [128, 2048], "float32"),
+}
+SEMAPHORES = (["sw", "ss", "sv", "sa", "swl", "ssn", "sso", "szo", "sk", "se", "sqe", "sdn", "sx1", "sx2", "sqm", "lol", "loc",
+               "la0", "la1", "la2", "ar0", "ar1", "ar2", "arn", "gv0", "gv1", "gv2", "gs0", "gs1", "gs2", "gov", "gos",
+               "sq0", "sq1", "sq2", "sqo", "tt", "hd2", "hd3", "sh", "sy", "yc4", "ym4"]
+              + ["%s%d" % (n, b) for n in ("m0", "m1", "m2", "mn", "c0", "c1", "c2", "cn", "gg", "tp", "hh", "hq", "ym", "yc") for b in range(4)])
+
+
+def rank_program(g, core, T, topo):
+    r = T.rank_of(core)
+    if r is None:
+        return
+    S = T.sem
+    v, s, te, sy = g.vector, g.scalar, g.tensor, g.sync
+    Copy = ActivationFunctionType.Copy
+    cores = T.cores
+
+    chips = []
+    for q in range(N):
+        if chips and topo.chip(cores[chips[-1][0]]) == topo.chip(cores[q]):
+            chips[-1].append(q)
+        else:
+            chips.append([q])
+    me = [k for k in range(len(chips)) if r in chips[k]][0]
+    pos = chips[me].index(r)
+    near = chips[me][1 - pos]
+    order = sorted((1, 2, 3), key=lambda x: topo.same_plane(topo.chip(core), topo.chip(cores[chips[me ^ x][0]])))
+    far = [chips[me ^ x] for x in order]
+    off = topo.engines(core, cores[far[0][0]])
+    for x in far:
+        off = [e for e in off if e in topo.engines(core, cores[x[0]])]
+    on = [e for e in topo.engines(core, cores[near]) if e not in off]
+    W = len(off) // 2
+
+    def msk(es):
+        return sum(1 << e for e in es)
+
+    def send(items, local):
+        tr = []
+        for q, es, src, dst, sem in items:
+            rid, pid, _ = topo.addr(cores[q])
+            tr.append(RemoteDMATransfer(dst_ids=[DstId(rid=rid, pnc=pid)], dma_engine_mask=msk(es), remote_sem=sem, src=src, dst=dst, alu_op=0))
+        g.remote_dma_fused(tr, local_sem=local)
+        return sum(len(it[1]) for it in items)
+
+    for k in range(8):
+        (sy if k % 2 == 0 else s).dma_start(out=T.wraw[16 * k:16 * k + 16, :], in_=T.want[:]).then_inc(S.sw, 16)
+    sy.dma_start(out=T.vt[:], in_=T.v[:]).then_inc(S.sv, 16)
+    for k in range(8):
+        s.dma_start(out=T.sraw[16 * k:16 * k + 16, :], in_=T.slot[:]).then_inc(S.ss, 16)
+
+    g.iota(T.kk[:], [[1, 128], [-1, 4]], 0, 0, allow_small_or_imprecise_dtypes=True).then_inc(S.sk, 1)
+    g.iota(T.kc[:], [[-128, 2]], 0, 4, allow_small_or_imprecise_dtypes=True).then_inc(S.sk, 1)
+    g.iota(T.kb[:], [[-1, 2], [-1, 4]], -256, 4, allow_small_or_imprecise_dtypes=True).then_inc(S.sk, 1)
+    g.iota(T.kd[:], [[1, 128]], 0, -1, allow_small_or_imprecise_dtypes=True).then_inc(S.sk, 1)
+    g.wait_ge(S.swl, 1)
+    left = 0
+    for k in range(3):
+        dst = T["l%d" % k]
+        it = [(q, off[W * i:W * i + W], T.wl[:, L * q:L * q + L], dst[:, L * pos:L * pos + L], S["la%d" % k]) for i, q in enumerate(far[k])]
+        if k == 1:
+            it.append((near, on[0:W // 2], T.wl[:, L * near:L * near + L], dst[:, 2 * L:3 * L], S.la1))
+        left += send(it, S.lol)
+    n0 = 0 if pos == 0 else 128
+    gone = 0
+    for k in range(3):
+        g.wait_ge(S["sq%d" % k], 1)
+        for what, mine, theirs, nn in (("codes", T["q%d" % k], T["r%d" % k], T.rn), ("scales", T["x%d" % k], T["rx%d" % k], T.rxn)):
+            def view(buf, a):
+                ap = buf[:, a:a + CAPP]
+                return ap.bitcast(dt.uint8) if what == "codes" else ap
+            it = [(q, off[W * i:W * i + W], view(mine, CAPP * i), view(theirs, CAPP * pos), S["ar%d" % k]) for i, q in enumerate(far[k])]
+            if k == 1:
+                it.append((near, on[0:W], view(mine, P2), view(nn, n0), S.arn))
+            gone += send(it, S.loc)
+    g.wait_ge(S.loc, gone)
+    sy.wait_ge(S.lol, left)
+    sy.dma_start(out=T.at[:], in_=T.a[:]).then_inc(S.sa, 16)
+
+    v.wait_ge(S.sw, 128)
+    v.tensor_scalar(T.wl[:], T.wraw[:], 0.0, 4.0, AluOpType.max, AluOpType.mult).then_inc(S.swl, 1)
+    o0 = 32 if pos == 0 else 0
+    v.memset(T.town[:, 0:128] if pos == 0 else T.town[:, 384:512], 0.0).then_inc(S.szo, 1)
+    v.wait_ge(S.sk, 4)
+    for b in range(2):
+        v.tensor_scalar(T.et[:, 512 * b:512 * b + 512], T.kk[:], T.kc[:, b:b + 1], None, AluOpType.is_equal).then_inc(S.se, 1)
+    for b in range(2):
+        for e in range(4):
+            v.tensor_scalar(T.et[:, 1024 + 512 * b + e:1536 + 512 * b:4], T.kk[:, e:512:4], 2.0, T.kb[:, 4 * b + e:4 * b + e + 1],
+                            AluOpType.mult, AluOpType.is_equal).then_inc(S.se, 1)
+    v.tensor_scalar(T.idn[:], T.kd[:], 0.0, None, AluOpType.is_equal).then_inc(S.sdn, 1)
+
+    v.wait_ge(S.sv, 16)
+    s.wait_ge(S.sv, 16)
+
+    def gather(wait, tile, n, offs, sv_, ss_):
+        v.wait_ge(*wait)
+        s.wait_ge(*wait)
+        for t in range(4):
+            out, in_ = tile[:, t:4 * n:4], T.vt[:, t:4096].indirect(offs)
+            if t < 2:
+                v.tensor_copy(out, in_).then_inc(sv_, 1)
+            else:
+                s.activation(out, in_, Copy).then_inc(ss_, 1)
+        v.wait_ge(sv_, 2)
+        v.wait_ge(ss_, 2)
+
+    for k in range(3):
+        n, came = (P2 + CAPP, 2 * W + W // 2) if k == 1 else (P2, 2 * W)
+        gather((S["la%d" % k], came), T["t%d" % k], n, T["l%d" % k][:], S["gv%d" % k], S["gs%d" % k])
+        v.quantize_mx(T["q%d" % k][:], T["x%d" % k][:], T["t%d" % k][:]).then_inc(S["sq%d" % k], 1)
+    v.wait_ge(S.se, 10)
+    v.quantize_mx(T.qe[:], T.xe[:], T.et[:]).then_inc(S.sqe, 1)
+    v.wait_ge(S.swl, 1)
+    s.wait_ge(S.swl, 1)
+    for t in range(4):
+        out, in_ = T.town[:, 4 * o0 + t:4 * (o0 + CAPP):4], T.vt[:, t:4096].indirect(T.wl[:, L * r:L * r + L])
+        if t < 2:
+            v.tensor_copy(out, in_).then_inc(S.gov, 1)
+        else:
+            s.activation(out, in_, Copy).then_inc(S.gos, 1)
+    v.wait_ge(S.gov, 2)
+    v.wait_ge(S.gos, 2)
+    v.wait_ge(S.szo, 1)
+    ow = 0 if pos == 0 else CAPP
+    v.quantize_mx(T.rn[:, ow:ow + 128], T.rxn[:, ow:ow + 128], T.town[:]).then_inc(S.sqo, 1)
+
+    v.wait_ge(S.ss, 128)
+    v.tensor_copy(T.sn[:], T.sraw[:]).then_inc(S.ssn, 1)
+    for u in range(2):
+        for k in range(2):
+            v.tensor_copy(T.sx[:, 32 * u + 16 * k:32 * u + 16 * k + 16], T.sraw[:, 16 * u:16 * u + 16]).then_inc(S.sx1, 1)
+    v.wait_ge(S.sx1, 4)
+    v.transpose(T.st[:], T.sx[:]).then_inc(S.sx2, 1)
+    v.wait_ge(S.sx2, 1)
+    for u in range(2):
+        for t in range(4):
+            v.tensor_copy(T.so[:, 8 * t + u:8 * t + 8:2], T.st[:, 32 * u + t:32 * u + 16:4]).then_inc(S.sso, 1)
+    v.wait_ge(S.sa, 16)
+    v.quantize_mx(T.qm[:], T.xm[:], T.at[:]).then_inc(S.sqm, 1)
+
+    te.wait_ge(S.sqe, 1)
+
+    def unpack(ps, q, x, a, name, before):
+        for b in range(4):
+            if before:
+                te.wait_ge(S["%s%d" % (before, b)], 1)
+            te.matmul_mx(ps[:, 512 * b:512 * b + P2], T.qe[:, 128 * b:128 * b + 128], T.xe[:, 128 * b:128 * b + 128],
+                         q[:, a:a + P2], x[:, a:a + P2], True, True).then_inc(S["%s%d" % (name, b)], 1)
+
+    te.wait_ge(S.ar0, 4 * W)
+    unpack(T.p0, T.r0, T.rx0, 0, "m0", None)
+    te.wait_ge(S.sqo, 1)
+    te.wait_ge(S.arn, 2 * W)
+    unpack(T.p1, T.rn, T.rxn, o0, "mn", None)
+    te.wait_ge(S.ar1, 4 * W)
+    unpack(T.p0, T.r1, T.rx1, 0, "m1", "c0")
+    te.wait_ge(S.ar2, 4 * W)
+    unpack(T.p1, T.r2, T.rx2, 0, "m2", "cn")
+
+    def copy(qu, out, in_, sem):
+        if qu is v:
+            v.tensor_copy(out, in_).then_inc(sem, 1)
+        else:
+            s.activation(out, in_, Copy).then_inc(sem, 1)
+
+    def queue(b):
+        return v if b % 2 == 0 else s
+
+    def store(qu, k, ps, ranks, b):
+        qu.wait_ge(S["m%s%d" % (k, b)], 1)
+        a = N * CAPP * b + CAPP * ranks[0]
+        copy(qu, T.win[:, a:a + P2], ps[:, 512 * b:512 * b + P2], S["c%s%d" % (k, b)])
+
+    def pick(b):
+        qu = queue(b)
+        qu.wait_ge(S.ssn if b < 2 else S.sso, 1 if b < 2 else 8)
+        for k in "0n12":
+            qu.wait_ge(S["c%s%d" % (k, b)], 1)
+        out, offs = (T.gf, T.sn) if b < 2 else (T.gb, T.so)
+        c = 512 * (b % 2)
+        copy(qu, out[:, c:c + 512], T.win[:, N * CAPP * b:N * CAPP * (b + 1)].indirect(offs[:]), S["gg%d" % b])
+
+    for b in range(4):
+        store(s, "0", T.p0, far[0], b)
+    for b in range(4):
+        store(s, "n", T.p1, chips[me], b)
+    for b in range(4):
+        store(queue(b), "1", T.p0, far[1], b)
+    for b in range(4):
+        store(queue(b), "2", T.p1, far[2], b)
+        pick(b)
+
+    te.wait_ge(S.sdn, 1)
+    for b in range(2):
+        te.wait_ge(S["gg%d" % b], 1)
+        for t in range(4):
+            te.transpose(T.p0[:, 512 * b + t:512 * b + 512:4], T.gf[:, 512 * b + t:512 * b + 512:4], T.idn[:]).then_inc(S["tp%d" % b], 1)
+        s.wait_ge(S["tp%d" % b], 4)
+        s.activation(T.ht[:, 512 * b:512 * b + 512], T.p0[:, 512 * b:512 * b + 512], Copy).then_inc(S["hh%d" % b], 1)
+    for b in (2, 3):
+        v.wait_ge(S["gg%d" % b], 1)
+        for t in range(4):
+            v.transpose(T.tr[:, 4 * (b - 2) + t:1024:8], T.gb[:, 512 * (b - 2) + 128 * t:512 * (b - 2) + 128 * t + 128]).then_inc(S.tt, 1)
+    sy.wait_ge(S.tt, 8)
+    for a in range(4):
+        sy.dma_start(out=T.ht[:, 1024 + 256 * a:1024 + 256 * a + 256], in_=T.tr[32 * a:32 * a + 32, :]).then_inc(S["hd%d" % (2 + a // 2)], 16)
+
+    def ready(qu, b):
+        if b < 2:
+            qu.wait_ge(S["hh%d" % b], 1)
+        else:
+            qu.wait_ge(S["hd%d" % b], 32)
+
+    parts = [(0, 0, 512, T.p0, 1024, s), (1, 0, 512, T.p0, 1536, s), (2, 0, 512, T.p1, 0, v), (3, 0, 256, T.p1, 512, s), (3, 256, 256, T.p1, 1024, v)]
+    for b in range(4):
+        ready(v, b)
+        v.quantize_mx(T.qh[:, 128 * b:128 * b + 128], T.xh[:, 128 * b:128 * b + 128], T.ht[:, 512 * b:512 * b + 512]).then_inc(S["hq%d" % b], 1)
+    te.wait_ge(S.sqm, 1)
+    for i, (b, a, n, ps, at, qu) in enumerate(parts):
+        te.wait_ge(S["hq%d" % b], 1)
+        te.matmul_mx(ps[:, at:at + n], T.qh[:, 128 * b:128 * b + 128], T.xh[:, 128 * b:128 * b + 128],
+                     T.qm[:, a:a + n], T.xm[:, a:a + n], True, True).then_inc(S["ym%d" % i], 1)
+        qu.wait_ge(S["ym%d" % i], 1)
+        copy(qu, T.yt[:, 512 * b + a:512 * b + a + n], ps[:, at:at + n], S["yc%d" % i])
+
+    for what, i in (("h", 0), ("h", 1), ("h", 2), ("h", 3), ("y", 0), ("y", 1), ("y", 2), ("y", 3), ("y", 4)):
+        if what == "h":
+            ready(sy, i)
+            sy.dma_start(out=T.h[:, 512 * i:512 * i + 512], in_=T.ht[:, 512 * i:512 * i + 512]).then_inc(S.sh, 16)
+        else:
+            b, a, n = parts[i][0:3]
+            c = slice(512 * b + a, 512 * b + a + n)
+            sy.wait_ge(S["yc%d" % i], 1)
+            sy.dma_start(out=T.y[:, c], in_=T.yt[:, c]).then_inc(S.sy, 16)
+    sy.wait_ge(S.sh, 64)
+    sy.wait_ge(S.sy, 80)

@@ -9,21 +9,24 @@ E4 = "float8_e4m3fn_x4"
 SCRATCH = {
     "wraw": ("sbuf", [128, N * L], "int32"), "wl": ("sbuf", [128, N * L], "uint16"),
     "sraw": ("sbuf", [128, 32], "int32"), "sn": ("sbuf", [128, 32], "uint16"), "so": ("sbuf", [128, 32], "uint16"),
+    "sf": ("sbuf", [128, 32], "float32"), "sg": ("sbuf", [128, 32], "float32"),
     "sx": ("sbuf", [128, 64], "float32"), "st": ("sbuf", [128, 64], "float32"),
-    "l0": ("sbuf", [128, 2 * L], "uint16"), "l1": ("sbuf", [128, 3 * L], "uint16"), "l2": ("sbuf", [128, 2 * L], "uint16"),
+    "l0": ("sbuf", [128, 2 * L], "uint16"), "l1": ("sbuf", [128, 2 * L], "uint16"), "l2": ("sbuf", [128, 2 * L], "uint16"),
+    "l3": ("sbuf", [128, 16], "uint16"),
     "vt": ("sbuf", [128, 4096], "bfloat16"), "at": ("sbuf", [128, 2048], "bfloat16"),
-    "t0": ("sbuf", [128, 4 * P2], "bfloat16"), "t1": ("sbuf", [128, 4 * (P2 + CAPP)], "bfloat16"), "t2": ("sbuf", [128, 4 * P2], "bfloat16"),
+    "t0": ("sbuf", [128, 4 * P2], "bfloat16"), "t1": ("sbuf", [128, 4 * P2], "bfloat16"),
+    "t2": ("sbuf", [128, 4 * P2], "bfloat16"), "t3": ("sbuf", [128, 4 * P2], "bfloat16"),
     "q0": ("sbuf", [128, P2], E4), "x0": ("sbuf", [128, P2], "uint8"),
-    "q1": ("sbuf", [128, P2 + CAPP], E4), "x1": ("sbuf", [128, P2 + CAPP], "uint8"),
+    "q1": ("sbuf", [128, P2], E4), "x1": ("sbuf", [128, P2], "uint8"),
     "q2": ("sbuf", [128, P2], E4), "x2": ("sbuf", [128, P2], "uint8"),
-    "town": ("sbuf", [128, 512], "bfloat16"),
+    "q3": ("sbuf", [128, 128], E4), "x3": ("sbuf", [128, 128], "uint8"),
+    "q4": ("sbuf", [128, 3 * CAPP], E4), "x4": ("sbuf", [128, 3 * CAPP], "uint8"),
+    "fl": ("sbuf", [128, L], "uint16"), "fq": ("sbuf", [128, P2], E4), "fx": ("sbuf", [128, P2], "uint8"),
     "r0": ("sbuf", [128, P2], E4), "rx0": ("sbuf", [128, P2], "uint8"),
     "r1": ("sbuf", [128, P2], E4), "rx1": ("sbuf", [128, P2], "uint8"),
     "r2": ("sbuf", [128, P2], E4), "rx2": ("sbuf", [128, P2], "uint8"),
-    "rn": ("sbuf", [128, 224], E4), "rxn": ("sbuf", [128, 224], "uint8"),
     "qm": ("sbuf", [128, 512], E4), "xm": ("sbuf", [128, 512], "uint8"),
-    "kk": ("sbuf", [128, 512], "bfloat16"), "kc": ("sbuf", [128, 2], "float32"), "kb": ("sbuf", [128, 8], "float32"),
-    "kd": ("sbuf", [128, 128], "float32"), "idn": ("sbuf", [128, 128], "float32"),
+    "k4": ("sbuf", [128, 256], "bfloat16"), "one": ("sbuf", [128, 128], "float32"), "idn": ("sbuf", [128, 128], "float32"),
     "et": ("sbuf", [128, 2048], "bfloat16"), "qe": ("sbuf", [128, 512], E4), "xe": ("sbuf", [128, 512], "uint8"),
     "win": ("sbuf", [128, 4 * N * CAPP], "bfloat16"),
     "gf": ("sbuf", [128, 1024], "float32"), "gb": ("sbuf", [128, 1024], "bfloat16"), "tr": ("sbuf", [128, 1024], "bfloat16"),
@@ -31,20 +34,28 @@ SCRATCH = {
     "yt": ("sbuf", [128, 2048], "float32"),
     "p0": ("psum", [128, 2048], "float32"), "p1": ("psum", [128, 2048], "float32"),
 }
-SEMAPHORES = (["sw", "ss", "sv", "sa", "swl", "ssn", "sso", "szo", "sk", "se", "sqe", "sdn", "sx1", "sx2", "sqm", "lol", "loc",
-               "la0", "la1", "la2", "ar0", "ar1", "ar2", "arn", "gv0", "gv1", "gv2", "gs0", "gs1", "gs2", "gov", "gos",
-               "sq0", "sq1", "sq2", "sqo", "tt", "hd2", "hd3", "sh", "sy", "yc4", "ym4"]
-              + ["%s%d" % (n, b) for n in ("m0", "m1", "m2", "mn", "c0", "c1", "c2", "cn", "gg", "tp", "hh", "hq", "ym", "yc") for b in range(4)])
+SEMAPHORES = (["sw", "ss", "sv", "sa", "swl", "ssn", "ssf", "ssg", "sso", "sx1", "sx2", "sk", "se", "sqe", "sqm", "sone", "sdn", "lol", "loc", "sent",
+               "ar0", "ar1", "ar2", "arn", "dl", "dq0", "dq1", "dx0", "dx1", "tt", "tp", "gv4", "gs4", "sq4", "sh", "sy", "yc4", "ym4", "yc5", "ym5"]
+              + ["%s%d" % (n, b) for n in ("la", "gv", "gs", "sq", "m0", "m1", "m2", "mn", "c0", "c1", "c2", "cn", "gg", "u", "hd", "hq", "ym", "yc")
+                 for b in range(4)])
 
 
 def rank_program(g, core, T, topo):
-    r = T.rank_of(core)
-    if r is None:
-        return
     S = T.sem
     v, s, te, sy = g.vector, g.scalar, g.tensor, g.sync
     Copy = ActivationFunctionType.Copy
     cores = T.cores
+
+    here = [c for c in cores if topo.chip(c) == topo.chip(core)]
+    if not here:
+        return
+    spare = [c for c in topo.cores_of(core) if c not in cores and topo.die(c) != topo.die(here[0]) and all(topo.may_write(c, d) for d in cores)]
+    if core in here:
+        r, helper = T.rank_of(core), spare[here.index(core)]
+    elif core in spare:
+        r, helper = T.rank_of(here[spare.index(core)]), None
+    else:
+        return
 
     chips = []
     for q in range(N):
@@ -62,138 +73,154 @@ def rank_program(g, core, T, topo):
         off = [e for e in off if e in topo.engines(core, cores[x[0]])]
     on = [e for e in topo.engines(core, cores[near]) if e not in off]
     W = len(off) // 2
+    side = on[0:W]
 
     def msk(es):
         return sum(1 << e for e in es)
 
     def send(items, local):
         tr = []
-        for q, es, src, dst, sem in items:
-            rid, pid, _ = topo.addr(cores[q])
+        for c, es, src, dst, sem in items:
+            rid, pid, _ = topo.addr(c)
             tr.append(RemoteDMATransfer(dst_ids=[DstId(rid=rid, pnc=pid)], dma_engine_mask=msk(es), remote_sem=sem, src=src, dst=dst, alu_op=0))
         g.remote_dma_fused(tr, local_sem=local)
         return sum(len(it[1]) for it in items)
 
-    for k in range(8):
+    def view(buf, a, codes):
+        ap = buf[:, a:a + CAPP]
+        return ap.bitcast(dt.uint8) if codes else ap
+
+    if helper is None:
+        g.wait_ge(S.dl, W)
+        gone = send([(cores[far[2][1 - pos]], off, T.fl[:], T.l3[:, 8 - L * pos:8 - L * pos + L], S.la3)], S.loc)
+        for k in range(2):
+            for n, codes in (("q", True), ("x", False)):
+                g.wait_ge(S["d%s%d" % (n, k)], len(on))
+                theirs = T[("r%d" if codes else "rx%d") % k]
+                gone += send([(cores[far[k][1 - pos]], off, view(T["f%s" % n], CAPP * k, codes), view(theirs, CAPP * pos, codes), S["ar%d" % k])], S.loc)
+        g.wait_ge(S.loc, gone)
+        return
+
+    for k in range(2):
         (sy if k % 2 == 0 else s).dma_start(out=T.wraw[16 * k:16 * k + 16, :], in_=T.want[:]).then_inc(S.sw, 16)
     sy.dma_start(out=T.vt[:], in_=T.v[:]).then_inc(S.sv, 16)
     for k in range(8):
         s.dma_start(out=T.sraw[16 * k:16 * k + 16, :], in_=T.slot[:]).then_inc(S.ss, 16)
 
-    g.iota(T.kk[:], [[1, 128], [-1, 4]], 0, 0, allow_small_or_imprecise_dtypes=True).then_inc(S.sk, 1)
-    g.iota(T.kc[:], [[-128, 2]], 0, 4, allow_small_or_imprecise_dtypes=True).then_inc(S.sk, 1)
-    g.iota(T.kb[:], [[-1, 2], [-1, 4]], -256, 4, allow_small_or_imprecise_dtypes=True).then_inc(S.sk, 1)
-    g.iota(T.kd[:], [[1, 128]], 0, -1, allow_small_or_imprecise_dtypes=True).then_inc(S.sk, 1)
-    g.wait_ge(S.swl, 1)
+    g.iota(T.k4[:], [[1, 256]], 0, -4, allow_small_or_imprecise_dtypes=True).then_inc(S.sk, 1)
+    g.wait_ge(S.swl, 4)
     left = 0
-    for k in range(3):
-        dst = T["l%d" % k]
-        it = [(q, off[W * i:W * i + W], T.wl[:, L * q:L * q + L], dst[:, L * pos:L * pos + L], S["la%d" % k]) for i, q in enumerate(far[k])]
-        if k == 1:
-            it.append((near, on[0:W // 2], T.wl[:, L * near:L * near + L], dst[:, 2 * L:3 * L], S.la1))
+
+    def wants(q):
+        return T.wl[:, L * q:L * q + L]
+
+    for k in range(2):
+        it = [(cores[q], off[W * i:W * i + W], wants(q), T["l%d" % k][:, L * pos:L * pos + L], S["la%d" % k]) for i, q in enumerate(far[k])]
+        if k == 0:
+            it.append((helper, side, wants(far[2][1 - pos]), T.fl[:], S.dl))
         left += send(it, S.lol)
-    n0 = 0 if pos == 0 else 128
+    left += send([(cores[far[2][pos]], off, wants(far[2][pos]), T.l2[:, 0:L], S.la2), (cores[near], on[W:2 * W], wants(near), T.l2[:, L:2 * L], S.la2)], S.lol)
+    g.wait_ge(S.sone, 1)
+    g.affine_select(T.idn[:], T.one[:], [[-1, 128]], AluOpType.is_equal, 0.0, 0, 1).then_inc(S.sdn, 1)
     gone = 0
-    for k in range(3):
+    for k in range(4):
         g.wait_ge(S["sq%d" % k], 1)
-        for what, mine, theirs, nn in (("codes", T["q%d" % k], T["r%d" % k], T.rn), ("scales", T["x%d" % k], T["rx%d" % k], T.rxn)):
-            def view(buf, a):
-                ap = buf[:, a:a + CAPP]
-                return ap.bitcast(dt.uint8) if what == "codes" else ap
-            it = [(q, off[W * i:W * i + W], view(mine, CAPP * i), view(theirs, CAPP * pos), S["ar%d" % k]) for i, q in enumerate(far[k])]
-            if k == 1:
-                it.append((near, on[0:W], view(mine, P2), view(nn, n0), S.arn))
+        for n, codes in (("q", True), ("x", False)):
+            mine = T["%s%d" % (n, k)]
+            theirs = view(T[("r%d" if codes else "rx%d") % min(k, 2)], CAPP * pos, codes)
+            if k < 2:
+                it = [(cores[far[k][pos]], off, view(mine, CAPP * pos, codes), theirs, S["ar%d" % k]),
+                      (helper, on, view(mine, CAPP * (1 - pos), codes), view(T["f%s" % n], CAPP * k, codes), S["d%s%d" % (n, k)])]
+            elif k == 2:
+                it = [(cores[far[2][pos]], off, view(mine, 0, codes), theirs, S.ar2),
+                      (cores[near], on, view(mine, CAPP, codes), view(T[n + "4"], P2 * pos, codes), S.arn)]
+            else:
+                it = [(cores[far[2][1 - pos]], off, view(mine, (128 - CAPP) * pos, codes), theirs, S.ar2)]
             gone += send(it, S.loc)
+    g.sem_inc(S.sent, 1)
+    g.wait_ge(S.lol, left)
     g.wait_ge(S.loc, gone)
-    sy.wait_ge(S.lol, left)
+    sy.wait_ge(S.sent, 1)
     sy.dma_start(out=T.at[:], in_=T.a[:]).then_inc(S.sa, 16)
 
-    v.wait_ge(S.sw, 128)
-    v.tensor_scalar(T.wl[:], T.wraw[:], 0.0, 4.0, AluOpType.max, AluOpType.mult).then_inc(S.swl, 1)
-    o0 = 32 if pos == 0 else 0
-    v.memset(T.town[:, 0:128] if pos == 0 else T.town[:, 384:512], 0.0).then_inc(S.szo, 1)
-    v.wait_ge(S.sk, 4)
-    for b in range(2):
-        v.tensor_scalar(T.et[:, 512 * b:512 * b + 512], T.kk[:], T.kc[:, b:b + 1], None, AluOpType.is_equal).then_inc(S.se, 1)
-    for b in range(2):
-        for e in range(4):
-            v.tensor_scalar(T.et[:, 1024 + 512 * b + e:1536 + 512 * b:4], T.kk[:, e:512:4], 2.0, T.kb[:, 4 * b + e:4 * b + e + 1],
-                            AluOpType.mult, AluOpType.is_equal).then_inc(S.se, 1)
-    v.tensor_scalar(T.idn[:], T.kd[:], 0.0, None, AluOpType.is_equal).then_inc(S.sdn, 1)
+    v.memset(T.et[:, 1025:1536:2], 0.0).then_inc(S.se, 1)
+    v.memset(T.et[:, 1536:2048:2], 0.0).then_inc(S.se, 1)
+    v.memset(T.one[:], 1.0).then_inc(S.sone, 1)
+    v.wait_ge(S.sk, 1)
+    for t in range(4):
+        if t == 1:
+            v.wait_ge(S.sw, 32)
+            for k in range(4):
+                v.tensor_scalar(T.wl[32 * k:32 * k + 32, :], T.wraw[0:32, :], 0.0, 4.0, AluOpType.max, AluOpType.mult).then_inc(S.swl, 1)
+        v.tensor_scalar(T.et[:, t:1024:4], T.k4[:], float(t), None, AluOpType.is_equal).then_inc(S.se, 1)
+    for b in (2, 3):
+        for u in range(2):
+            v.tensor_scalar(T.et[:, 512 * b + b % 2 + 2 * u:512 * b + 512:4], T.k4[:, 0:256:2], float(2 * u - 256), None,
+                            AluOpType.is_equal).then_inc(S.se, 1)
+    v.wait_ge(S.se, 10)
+    v.quantize_mx(T.qe[:], T.xe[:], T.et[:]).then_inc(S.sqe, 1)
+    v.wait_ge(S.swl, 4)
+    v.tensor_copy(T.l3[:, 8 - L * pos:8 - L * pos + L], wants(r)).then_inc(S.la3, 1)
 
     v.wait_ge(S.sv, 16)
     s.wait_ge(S.sv, 16)
+    rest = P2 - 128
+    phases = [(0, 0, P2, 0, 0, P2, 0), (1, 0, P2, 64, 0, P2, 0), (2, 0, P2, 64, 0, P2, 0),
+              (3, rest * pos, rest * pos + 128, 32, rest * pos, rest * pos + 128, 0),
+              (3, 128 * (1 - pos), 128 * (1 - pos) + rest, 0, rest * (1 - pos), rest * (1 - pos) + 128, CAPP - 32 * (1 - pos))]
+    for k, (j, a, b, part, qa, qb, to) in enumerate(phases):
+        def take(t, a, b):
+            o = 8 - L if j == 3 else 0
+            return T["t%d" % j][:, 4 * a + t:4 * b:4], T.vt[:, t:4096].indirect(T["l%d" % j][:, o + a // 16:o + b // 16])
+        for qu in (v, s):
+            qu.wait_ge(S["la%d" % j], (2 * W, 2 * W, 3 * W, 2 * W + 1)[j])
+        v.tensor_copy(*take(0, a, b)).then_inc(S["gv%d" % k], 1)
+        v.tensor_copy(*take(1, a, b - part)).then_inc(S["gv%d" % k], 1)
+        for out, in_ in [take(2, a, b), take(3, a, b)] + ([take(1, b - part, b)] if part else []):
+            s.activation(out, in_, Copy).then_inc(S["gs%d" % k], 1)
+        v.wait_ge(S["gv%d" % k], 2)
+        v.wait_ge(S["gs%d" % k], 3 if part else 2)
+        v.quantize_mx(T["q%d" % k][:, to:to + qb - qa], T["x%d" % k][:, to:to + qb - qa], T["t%d" % j][:, 4 * qa:4 * qb]).then_inc(S["sq%d" % k], 1)
+        if k == 3:
+            v.wait_ge(S.ss, 128)
+            v.tensor_copy(T.sf[:], T.sraw[:]).then_inc(S.ssf, 1)
 
-    def gather(wait, tile, n, offs, sv_, ss_):
-        v.wait_ge(*wait)
-        s.wait_ge(*wait)
-        for t in range(4):
-            out, in_ = tile[:, t:4 * n:4], T.vt[:, t:4096].indirect(offs)
-            if t < 2:
-                v.tensor_copy(out, in_).then_inc(sv_, 1)
-            else:
-                s.activation(out, in_, Copy).then_inc(ss_, 1)
-        v.wait_ge(sv_, 2)
-        v.wait_ge(ss_, 2)
-
-    for k in range(3):
-        n, came = (P2 + CAPP, 2 * W + W // 2) if k == 1 else (P2, 2 * W)
-        gather((S["la%d" % k], came), T["t%d" % k], n, T["l%d" % k][:], S["gv%d" % k], S["gs%d" % k])
-        v.quantize_mx(T["q%d" % k][:], T["x%d" % k][:], T["t%d" % k][:]).then_inc(S["sq%d" % k], 1)
-    v.wait_ge(S.se, 10)
-    v.quantize_mx(T.qe[:], T.xe[:], T.et[:]).then_inc(S.sqe, 1)
-    v.wait_ge(S.swl, 1)
-    s.wait_ge(S.swl, 1)
-    for t in range(4):
-        out, in_ = T.town[:, 4 * o0 + t:4 * (o0 + CAPP):4], T.vt[:, t:4096].indirect(T.wl[:, L * r:L * r + L])
-        if t < 2:
-            v.tensor_copy(out, in_).then_inc(S.gov, 1)
-        else:
-            s.activation(out, in_, Copy).then_inc(S.gos, 1)
-    v.wait_ge(S.gov, 2)
-    v.wait_ge(S.gos, 2)
-    v.wait_ge(S.szo, 1)
-    ow = 0 if pos == 0 else CAPP
-    v.quantize_mx(T.rn[:, ow:ow + 128], T.rxn[:, ow:ow + 128], T.town[:]).then_inc(S.sqo, 1)
-
-    v.wait_ge(S.ss, 128)
-    v.tensor_copy(T.sn[:], T.sraw[:]).then_inc(S.ssn, 1)
+    s.wait_ge(S.ssf, 1)
     for u in range(2):
-        for k in range(2):
-            v.tensor_copy(T.sx[:, 32 * u + 16 * k:32 * u + 16 * k + 16], T.sraw[:, 16 * u:16 * u + 16]).then_inc(S.sx1, 1)
+        for w in range(2):
+            s.activation(T.sx[:, 32 * u + 16 * w:32 * u + 16 * w + 16], T.sf[:, 16 * u:16 * u + 16], Copy).then_inc(S.sx1, 1)
     v.wait_ge(S.sx1, 4)
     v.transpose(T.st[:], T.sx[:]).then_inc(S.sx2, 1)
-    v.wait_ge(S.sx2, 1)
+    s.wait_ge(S.sx2, 1)
     for u in range(2):
         for t in range(4):
-            v.tensor_copy(T.so[:, 8 * t + u:8 * t + 8:2], T.st[:, 32 * u + t:32 * u + 16:4]).then_inc(S.sso, 1)
-    v.wait_ge(S.sa, 16)
-    v.quantize_mx(T.qm[:], T.xm[:], T.at[:]).then_inc(S.sqm, 1)
+            s.activation(T.sg[:, 8 * t + u:8 * t + 8:2], T.st[:, 32 * u + t:32 * u + 16:4], Copy).then_inc(S.ssg, 1)
+    v.tensor_copy(T.sn[:], T.sraw[:]).then_inc(S.ssn, 1)
 
     te.wait_ge(S.sqe, 1)
 
     def unpack(ps, q, x, a, name, before):
-        for b in range(4):
+        for b in (0, 2, 3, 1) if name == "m2" else range(4):
             if before:
                 te.wait_ge(S["%s%d" % (before, b)], 1)
             te.matmul_mx(ps[:, 512 * b:512 * b + P2], T.qe[:, 128 * b:128 * b + 128], T.xe[:, 128 * b:128 * b + 128],
                          q[:, a:a + P2], x[:, a:a + P2], True, True).then_inc(S["%s%d" % (name, b)], 1)
 
-    te.wait_ge(S.ar0, 4 * W)
+    te.wait_ge(S.ar0, 8 * W)
     unpack(T.p0, T.r0, T.rx0, 0, "m0", None)
-    te.wait_ge(S.sqo, 1)
-    te.wait_ge(S.arn, 2 * W)
-    unpack(T.p1, T.rn, T.rxn, o0, "mn", None)
-    te.wait_ge(S.ar1, 4 * W)
+    te.wait_ge(S.sq4, 1)
+    te.wait_ge(S.arn, 2 * len(on))
+    unpack(T.p1, T.q4, T.x4, CAPP * (1 - pos), "mn", None)
+    te.wait_ge(S.ar1, 8 * W)
     unpack(T.p0, T.r1, T.rx1, 0, "m1", "c0")
-    te.wait_ge(S.ar2, 4 * W)
+    te.wait_ge(S.ar2, 8 * W)
     unpack(T.p1, T.r2, T.rx2, 0, "m2", "cn")
 
-    def copy(qu, out, in_, sem):
+    def copy(qu, out, in_, sem, n=1):
         if qu is v:
-            v.tensor_copy(out, in_).then_inc(sem, 1)
+            v.tensor_copy(out, in_).then_inc(sem, n)
         else:
-            s.activation(out, in_, Copy).then_inc(sem, 1)
+            s.activation(out, in_, Copy).then_inc(sem, n)
 
     def queue(b):
         return v if b % 2 == 0 else s
@@ -203,49 +230,61 @@ def rank_program(g, core, T, topo):
         a = N * CAPP * b + CAPP * ranks[0]
         copy(qu, T.win[:, a:a + P2], ps[:, 512 * b:512 * b + P2], S["c%s%d" % (k, b)])
 
-    def pick(b):
-        qu = queue(b)
-        qu.wait_ge(S.ssn if b < 2 else S.sso, 1 if b < 2 else 8)
+    def pick(qu, b, a, n, sem):
+        qu.wait_ge(S.ssn if b < 2 else S.sso, 1)
         for k in "0n12":
             qu.wait_ge(S["c%s%d" % (k, b)], 1)
         out, offs = (T.gf, T.sn) if b < 2 else (T.gb, T.so)
-        c = 512 * (b % 2)
-        copy(qu, out[:, c:c + 512], T.win[:, N * CAPP * b:N * CAPP * (b + 1)].indirect(offs[:]), S["gg%d" % b])
+        c = 512 * (b % 2) + a
+        copy(qu, out[:, c:c + n], T.win[:, N * CAPP * b:N * CAPP * (b + 1)].indirect(offs[:, a // 16:(a + n) // 16]), sem)
 
-    for b in range(4):
-        store(s, "0", T.p0, far[0], b)
-    for b in range(4):
-        store(s, "n", T.p1, chips[me], b)
-    for b in range(4):
-        store(queue(b), "1", T.p0, far[1], b)
-    for b in range(4):
-        store(queue(b), "2", T.p1, far[2], b)
-        pick(b)
+    def turn(b, ts, sem):
+        v.wait_ge(sem, 1)
+        for t in ts:
+            c = 512 * (b % 2) + 128 * t
+            v.transpose(T.tr[:, 4 * (b % 2) + t:1024:8], T.gb[:, c:c + 128]).then_inc(S.tt, 1)
 
-    te.wait_ge(S.sdn, 1)
-    for b in range(2):
-        te.wait_ge(S["gg%d" % b], 1)
-        for t in range(4):
-            te.transpose(T.p0[:, 512 * b + t:512 * b + 512:4], T.gf[:, 512 * b + t:512 * b + 512:4], T.idn[:]).then_inc(S["tp%d" % b], 1)
-        s.wait_ge(S["tp%d" % b], 4)
-        s.activation(T.ht[:, 512 * b:512 * b + 512], T.p0[:, 512 * b:512 * b + 512], Copy).then_inc(S["hh%d" % b], 1)
-    for b in (2, 3):
-        v.wait_ge(S["gg%d" % b], 1)
-        for t in range(4):
-            v.transpose(T.tr[:, 4 * (b - 2) + t:1024:8], T.gb[:, 512 * (b - 2) + 128 * t:512 * (b - 2) + 128 * t + 128]).then_inc(S.tt, 1)
+    for k, ps, ranks in (("0", T.p0, far[0]), ("n", T.p1, chips[me]), ("1", T.p0, far[1])):
+        for b in range(4):
+            store(queue(b), k, ps, ranks, b)
+        if k == "n":
+            v.wait_ge(S.ssg, 8)
+            v.tensor_copy(T.so[:], T.sg[:]).then_inc(S.sso, 1)
+    store(v, "2", T.p1, far[2], 0)
+    pick(v, 0, 0, 512, S.gg0)
+    store(s, "2", T.p1, far[2], 2)
+    store(s, "2", T.p1, far[2], 3)
+    pick(s, 3, 0, 512, S.gg3)
+    pick(v, 2, 0, 512, S.gg2)
+    store(s, "2", T.p1, far[2], 1)
+    pick(s, 1, 0, 512, S.gg1)
+    turn(2, range(4), S.gg2)
+    turn(3, range(4), S.gg3)
+    v.wait_ge(S.sa, 16)
+    v.quantize_mx(T.qm[:], T.xm[:], T.at[:]).then_inc(S.sqm, 1)
     sy.wait_ge(S.tt, 8)
     for a in range(4):
-        sy.dma_start(out=T.ht[:, 1024 + 256 * a:1024 + 256 * a + 256], in_=T.tr[32 * a:32 * a + 32, :]).then_inc(S["hd%d" % (2 + a // 2)], 16)
+        c = 1024 + 256 * a
+        sy.dma_start(out=T.ht[:, c:c + 256], in_=T.tr[32 * a:32 * a + 32, :]).then_inc(S["hd%d" % (2 + a // 2)], 16)
 
-    def ready(qu, b):
-        if b < 2:
-            qu.wait_ge(S["hh%d" % b], 1)
-        else:
-            qu.wait_ge(S["hd%d" % b], 32)
+    for sem in (S.sdn, S.gg0):
+        te.wait_ge(sem, 1)
+    for t in range(4):
+        te.transpose(T.p0[:, t:512:4], T.gf[:, t:512:4], T.idn[:]).then_inc(S.tp, 1)
+    s.wait_ge(S.tp, 4)
+    copy(s, T.ht[:, 0:512], T.p0[:, 0:512], S.hd0, 32)
+    for sem in (S.gg1, S.c11, S.c12, S.c13, S.c22):
+        te.wait_ge(sem, 1)
+    for t in range(4):
+        bank = T.p0[:, 512 * t + 512:512 * t + 640] if t < 3 else T.p1[:, 1024:1152]
+        te.transpose(bank, T.gf[:, 512 + t:1024:4], T.idn[:]).then_inc(S["u%d" % t], 1)
+        s.wait_ge(S["u%d" % t], 1)
+        copy(s, T.ht[:, 512 + t:1024:4], bank, S.hd1, 8)
 
-    parts = [(0, 0, 512, T.p0, 1024, s), (1, 0, 512, T.p0, 1536, s), (2, 0, 512, T.p1, 0, v), (3, 0, 256, T.p1, 512, s), (3, 256, 256, T.p1, 1024, v)]
-    for b in range(4):
-        ready(v, b)
+    parts = [(0, 0, 512, T.p1, 0, s), (2, 0, 512, T.p1, 1536, v), (1, 0, 256, T.p1, 512, s), (1, 256, 256, T.p0, 0, s),
+             (3, 0, 256, T.p0, 512, v), (3, 256, 256, T.p0, 1024, s)]
+    for b in (0, 2, 1, 3):
+        v.wait_ge(S["hd%d" % b], 32)
         v.quantize_mx(T.qh[:, 128 * b:128 * b + 128], T.xh[:, 128 * b:128 * b + 128], T.ht[:, 512 * b:512 * b + 512]).then_inc(S["hq%d" % b], 1)
     te.wait_ge(S.sqm, 1)
     for i, (b, a, n, ps, at, qu) in enumerate(parts):
@@ -255,9 +294,9 @@ def rank_program(g, core, T, topo):
         qu.wait_ge(S["ym%d" % i], 1)
         copy(qu, T.yt[:, 512 * b + a:512 * b + a + n], ps[:, at:at + n], S["yc%d" % i])
 
-    for what, i in (("h", 0), ("h", 1), ("h", 2), ("h", 3), ("y", 0), ("y", 1), ("y", 2), ("y", 3), ("y", 4)):
+    for what, i in [("h", b) for b in (0, 2, 1, 3)] + [("y", i) for i in range(len(parts))]:
         if what == "h":
-            ready(sy, i)
+            sy.wait_ge(S["hd%d" % i], 32)
             sy.dma_start(out=T.h[:, 512 * i:512 * i + 512], in_=T.ht[:, 512 * i:512 * i + 512]).then_inc(S.sh, 16)
         else:
             b, a, n = parts[i][0:3]
@@ -265,4 +304,4 @@ def rank_program(g, core, T, topo):
             sy.wait_ge(S["yc%d" % i], 1)
             sy.dma_start(out=T.y[:, c], in_=T.yt[:, c]).then_inc(S.sy, 16)
     sy.wait_ge(S.sh, 64)
-    sy.wait_ge(S.sy, 80)
+    sy.wait_ge(S.sy, 16 * len(parts))

from concourse.bass import DstId, RemoteDMATransfer
from concourse.mybir import dt, AluOpType, ActivationFunctionType

N, CAPP = 8, 96
L = CAPP // 16
P2 = 2 * CAPP
E4 = "float8_e4m3fn_x4"

SCRATCH = {
    "wraw": ("sbuf", [128, N * L], "int32"), "wl": ("sbuf", [128, N * L], "uint16"),
    "sraw": ("sbuf", [128, 32], "int32"), "sn": ("sbuf", [128, 32], "uint16"), "so": ("sbuf", [128, 32], "uint16"),
    "sf": ("sbuf", [128, 32], "float32"), "sg": ("sbuf", [128, 32], "float32"),
    "sx": ("sbuf", [128, 64], "float32"), "st": ("sbuf", [128, 64], "float32"),
    "l0": ("sbuf", [128, 2 * L], "uint16"), "l1": ("sbuf", [128, 2 * L], "uint16"), "l2": ("sbuf", [128, 2 * L], "uint16"),
    "l3": ("sbuf", [128, 16], "uint16"),
    "vt": ("sbuf", [128, 4096], "bfloat16"), "at": ("sbuf", [128, 2048], "bfloat16"),
    "t0": ("sbuf", [128, 4 * P2], "bfloat16"), "t1": ("sbuf", [128, 4 * P2], "bfloat16"),
    "t2": ("sbuf", [128, 4 * P2], "bfloat16"), "t3": ("sbuf", [128, 4 * P2], "bfloat16"),
    "q0": ("sbuf", [128, P2], E4), "x0": ("sbuf", [128, P2], "uint8"),
    "q1": ("sbuf", [128, P2], E4), "x1": ("sbuf", [128, P2], "uint8"),
    "q2": ("sbuf", [128, P2], E4), "x2": ("sbuf", [128, P2], "uint8"),
    "q3": ("sbuf", [128, 128], E4), "x3": ("sbuf", [128, 128], "uint8"),
    "q4": ("sbuf", [128, 3 * CAPP], E4), "x4": ("sbuf", [128, 3 * CAPP], "uint8"),
    "fl": ("sbuf", [128, L], "uint16"), "fq": ("sbuf", [128, P2], E4), "fx": ("sbuf", [128, P2], "uint8"),
    "r0": ("sbuf", [128, P2], E4), "rx0": ("sbuf", [128, P2], "uint8"),
    "r1": ("sbuf", [128, P2], E4), "rx1": ("sbuf", [128, P2], "uint8"),
    "r2": ("sbuf", [128, P2], E4), "rx2": ("sbuf", [128, P2], "uint8"),
    "qm": ("sbuf", [128, 512], E4), "xm": ("sbuf", [128, 512], "uint8"),
    "k4": ("sbuf", [128, 256], "bfloat16"), "one": ("sbuf", [128, 128], "float32"), "idn": ("sbuf", [128, 128], "float32"),
    "et": ("sbuf", [128, 2048], "bfloat16"), "qe": ("sbuf", [128, 512], E4), "xe": ("sbuf", [128, 512], "uint8"),
    "win": ("sbuf", [128, 4 * N * CAPP], "bfloat16"),
    "gf": ("sbuf", [128, 1024], "float32"), "gb": ("sbuf", [128, 1024], "bfloat16"), "tr": ("sbuf", [128, 1024], "bfloat16"),
    "ht": ("sbuf", [128, 2048], "bfloat16"), "qh": ("sbuf", [128, 512], E4), "xh": ("sbuf", [128, 512], "uint8"),
    "yt": ("sbuf", [128, 2048], "float32"),
    "p0": ("psum", [128, 2048], "float32"), "p1": ("psum", [128, 2048], "float32"),
}
SEMAPHORES = (["sw", "ss", "sv", "sa", "swl", "ssn", "ssf", "ssg", "sso", "sx1", "sx2", "sk", "se", "sqe", "sqm", "sone", "sdn", "lol", "loc", "sent",
               "ar0", "ar1", "ar2", "arn", "dl", "dq0", "dq1", "dx0", "dx1", "tt", "tp", "gv4", "gs4", "sq4", "sh", "sy", "yc4", "ym4", "yc5", "ym5"]
              + ["%s%d" % (n, b) for n in ("la", "gv", "gs", "sq", "m0", "m1", "m2", "mn", "c0", "c1", "c2", "cn", "gg", "u", "hd", "hq", "ym", "yc")
                 for b in range(4)])


def rank_program(g, core, T, topo):
    S = T.sem
    v, s, te, sy = g.vector, g.scalar, g.tensor, g.sync
    Copy = ActivationFunctionType.Copy
    cores = T.cores

    here = [c for c in cores if topo.chip(c) == topo.chip(core)]
    if not here:
        return
    spare = [c for c in topo.cores_of(core) if c not in cores and topo.die(c) != topo.die(here[0]) and all(topo.may_write(c, d) for d in cores)]
    if core in here:
        r, helper = T.rank_of(core), spare[here.index(core)]
    elif core in spare:
        r, helper = T.rank_of(here[spare.index(core)]), None
    else:
        return

    chips = []
    for q in range(N):
        if chips and topo.chip(cores[chips[-1][0]]) == topo.chip(cores[q]):
            chips[-1].append(q)
        else:
            chips.append([q])
    me = [k for k in range(len(chips)) if r in chips[k]][0]
    pos = chips[me].index(r)
    near = chips[me][1 - pos]
    order = sorted((1, 2, 3), key=lambda x: topo.same_plane(topo.chip(core), topo.chip(cores[chips[me ^ x][0]])))
    far = [chips[me ^ x] for x in order]
    off = topo.engines(core, cores[far[0][0]])
    for x in far:
        off = [e for e in off if e in topo.engines(core, cores[x[0]])]
    on = [e for e in topo.engines(core, cores[near]) if e not in off]
    W = len(off) // 2
    side = on[0:W]

    def msk(es):
        return sum(1 << e for e in es)

    def send(items, local):
        tr = []
        for c, es, src, dst, sem in items:
            rid, pid, _ = topo.addr(c)
            tr.append(RemoteDMATransfer(dst_ids=[DstId(rid=rid, pnc=pid)], dma_engine_mask=msk(es), remote_sem=sem, src=src, dst=dst, alu_op=0))
        g.remote_dma_fused(tr, local_sem=local)
        return sum(len(it[1]) for it in items)

    def view(buf, a, codes):
        ap = buf[:, a:a + CAPP]
        return ap.bitcast(dt.uint8) if codes else ap

    if helper is None:
        g.wait_ge(S.dl, W)
        gone = send([(cores[far[2][1 - pos]], off, T.fl[:], T.l3[:, 8 - L * pos:8 - L * pos + L], S.la3)], S.loc)
        for k in range(2):
            for n, codes in (("q", True), ("x", False)):
                g.wait_ge(S["d%s%d" % (n, k)], len(on))
                theirs = T[("r%d" if codes else "rx%d") % k]
                gone += send([(cores[far[k][1 - pos]], off, view(T["f%s" % n], CAPP * k, codes), view(theirs, CAPP * pos, codes), S["ar%d" % k])], S.loc)
        g.wait_ge(S.loc, gone)
        return

    for k in range(2):
        (sy if k % 2 == 0 else s).dma_start(out=T.wraw[16 * k:16 * k + 16, :], in_=T.want[:]).then_inc(S.sw, 16)
    sy.dma_start(out=T.vt[:], in_=T.v[:]).then_inc(S.sv, 16)
    for k in range(8):
        s.dma_start(out=T.sraw[16 * k:16 * k + 16, :], in_=T.slot[:]).then_inc(S.ss, 16)

    g.iota(T.k4[:], [[1, 256]], 0, -4, allow_small_or_imprecise_dtypes=True).then_inc(S.sk, 1)
    g.wait_ge(S.swl, 4)
    left = 0

    def wants(q):
        return T.wl[:, L * q:L * q + L]

    for k in range(2):
        it = [(cores[q], off[W * i:W * i + W], wants(q), T["l%d" % k][:, L * pos:L * pos + L], S["la%d" % k]) for i, q in enumerate(far[k])]
        if k == 0:
            it.append((helper, side, wants(far[2][1 - pos]), T.fl[:], S.dl))
        left += send(it, S.lol)
    left += send([(cores[far[2][pos]], off, wants(far[2][pos]), T.l2[:, 0:L], S.la2), (cores[near], on[W:2 * W], wants(near), T.l2[:, L:2 * L], S.la2)], S.lol)
    g.wait_ge(S.sone, 1)
    g.affine_select(T.idn[:], T.one[:], [[-1, 128]], AluOpType.is_equal, 0.0, 0, 1).then_inc(S.sdn, 1)
    gone = 0
    for k in range(4):
        g.wait_ge(S["sq%d" % k], 1)
        for n, codes in (("q", True), ("x", False)):
            mine = T["%s%d" % (n, k)]
            theirs = view(T[("r%d" if codes else "rx%d") % min(k, 2)], CAPP * pos, codes)
            if k < 2:
                it = [(cores[far[k][pos]], off, view(mine, CAPP * pos, codes), theirs, S["ar%d" % k]),
                      (helper, on, view(mine, CAPP * (1 - pos), codes), view(T["f%s" % n], CAPP * k, codes), S["d%s%d" % (n, k)])]
            elif k == 2:
                it = [(cores[far[2][pos]], off, view(mine, 0, codes), theirs, S.ar2),
                      (cores[near], on, view(mine, CAPP, codes), view(T[n + "4"], P2 * pos, codes), S.arn)]
            else:
                it = [(cores[far[2][1 - pos]], off, view(mine, (128 - CAPP) * pos, codes), theirs, S.ar2)]
            gone += send(it, S.loc)
    g.sem_inc(S.sent, 1)
    g.wait_ge(S.lol, left)
    g.wait_ge(S.loc, gone)
    sy.wait_ge(S.sent, 1)
    sy.dma_start(out=T.at[:], in_=T.a[:]).then_inc(S.sa, 16)

    v.memset(T.et[:, 1025:1536:2], 0.0).then_inc(S.se, 1)
    v.memset(T.et[:, 1536:2048:2], 0.0).then_inc(S.se, 1)
    v.memset(T.one[:], 1.0).then_inc(S.sone, 1)
    v.wait_ge(S.sk, 1)
    for t in range(4):
        if t == 1:
            v.wait_ge(S.sw, 32)
            for k in range(4):
                v.tensor_scalar(T.wl[32 * k:32 * k + 32, :], T.wraw[0:32, :], 0.0, 4.0, AluOpType.max, AluOpType.mult).then_inc(S.swl, 1)
        v.tensor_scalar(T.et[:, t:1024:4], T.k4[:], float(t), None, AluOpType.is_equal).then_inc(S.se, 1)
    for b in (2, 3):
        for u in range(2):
            v.tensor_scalar(T.et[:, 512 * b + b % 2 + 2 * u:512 * b + 512:4], T.k4[:, 0:256:2], float(2 * u - 256), None,
                            AluOpType.is_equal).then_inc(S.se, 1)
    v.wait_ge(S.se, 10)
    v.quantize_mx(T.qe[:], T.xe[:], T.et[:]).then_inc(S.sqe, 1)
    v.wait_ge(S.swl, 4)
    v.tensor_copy(T.l3[:, 8 - L * pos:8 - L * pos + L], wants(r)).then_inc(S.la3, 1)

    v.wait_ge(S.sv, 16)
    s.wait_ge(S.sv, 16)
    rest = P2 - 128
    phases = [(0, 0, P2, 0, 0, P2, 0), (1, 0, P2, 64, 0, P2, 0), (2, 0, P2, 64, 0, P2, 0),
              (3, rest * pos, rest * pos + 128, 32, rest * pos, rest * pos + 128, 0),
              (3, 128 * (1 - pos), 128 * (1 - pos) + rest, 0, rest * (1 - pos), rest * (1 - pos) + 128, CAPP - 32 * (1 - pos))]
    for k, (j, a, b, part, qa, qb, to) in enumerate(phases):
        def take(t, a, b):
            o = 8 - L if j == 3 else 0
            return T["t%d" % j][:, 4 * a + t:4 * b:4], T.vt[:, t:4096].indirect(T["l%d" % j][:, o + a // 16:o + b // 16])
        for qu in (v, s):
            qu.wait_ge(S["la%d" % j], (2 * W, 2 * W, 3 * W, 2 * W + 1)[j])
        v.tensor_copy(*take(0, a, b)).then_inc(S["gv%d" % k], 1)
        v.tensor_copy(*take(1, a, b - part)).then_inc(S["gv%d" % k], 1)
        for out, in_ in [take(2, a, b), take(3, a, b)] + ([take(1, b - part, b)] if part else []):
            s.activation(out, in_, Copy).then_inc(S["gs%d" % k], 1)
        v.wait_ge(S["gv%d" % k], 2)
        v.wait_ge(S["gs%d" % k], 3 if part else 2)
        v.quantize_mx(T["q%d" % k][:, to:to + qb - qa], T["x%d" % k][:, to:to + qb - qa], T["t%d" % j][:, 4 * qa:4 * qb]).then_inc(S["sq%d" % k], 1)
        if k == 3:
            v.wait_ge(S.ss, 128)
            v.tensor_copy(T.sf[:], T.sraw[:]).then_inc(S.ssf, 1)

    s.wait_ge(S.ssf, 1)
    for u in range(2):
        for w in range(2):
            s.activation(T.sx[:, 32 * u + 16 * w:32 * u + 16 * w + 16], T.sf[:, 16 * u:16 * u + 16], Copy).then_inc(S.sx1, 1)
    v.wait_ge(S.sx1, 4)
    v.transpose(T.st[:], T.sx[:]).then_inc(S.sx2, 1)
    s.wait_ge(S.sx2, 1)
    for u in range(2):
        for t in range(4):
            s.activation(T.sg[:, 8 * t + u:8 * t + 8:2], T.st[:, 32 * u + t:32 * u + 16:4], Copy).then_inc(S.ssg, 1)
    v.tensor_copy(T.sn[:], T.sraw[:]).then_inc(S.ssn, 1)

    te.wait_ge(S.sqe, 1)

    def unpack(ps, q, x, a, name, before):
        for b in (0, 2, 3, 1) if name == "m2" else range(4):
            if before:
                te.wait_ge(S["%s%d" % (before, b)], 1)
            te.matmul_mx(ps[:, 512 * b:512 * b + P2], T.qe[:, 128 * b:128 * b + 128], T.xe[:, 128 * b:128 * b + 128],
                         q[:, a:a + P2], x[:, a:a + P2], True, True).then_inc(S["%s%d" % (name, b)], 1)

    te.wait_ge(S.ar0, 8 * W)
    unpack(T.p0, T.r0, T.rx0, 0, "m0", None)
    te.wait_ge(S.sq4, 1)
    te.wait_ge(S.arn, 2 * len(on))
    unpack(T.p1, T.q4, T.x4, CAPP * (1 - pos), "mn", None)
    te.wait_ge(S.ar1, 8 * W)
    unpack(T.p0, T.r1, T.rx1, 0, "m1", "c0")
    te.wait_ge(S.ar2, 8 * W)
    unpack(T.p1, T.r2, T.rx2, 0, "m2", "cn")

    def copy(qu, out, in_, sem, n=1):
        if qu is v:
            v.tensor_copy(out, in_).then_inc(sem, n)
        else:
            s.activation(out, in_, Copy).then_inc(sem, n)

    def queue(b):
        return v if b % 2 == 0 else s

    def store(qu, k, ps, ranks, b):
        qu.wait_ge(S["m%s%d" % (k, b)], 1)
        a = N * CAPP * b + CAPP * ranks[0]
        copy(qu, T.win[:, a:a + P2], ps[:, 512 * b:512 * b + P2], S["c%s%d" % (k, b)])

    def pick(qu, b, a, n, sem):
        qu.wait_ge(S.ssn if b < 2 else S.sso, 1)
        for k in "0n12":
            qu.wait_ge(S["c%s%d" % (k, b)], 1)
        out, offs = (T.gf, T.sn) if b < 2 else (T.gb, T.so)
        c = 512 * (b % 2) + a
        copy(qu, out[:, c:c + n], T.win[:, N * CAPP * b:N * CAPP * (b + 1)].indirect(offs[:, a // 16:(a + n) // 16]), sem)

    def turn(b, ts, sem):
        v.wait_ge(sem, 1)
        for t in ts:
            c = 512 * (b % 2) + 128 * t
            v.transpose(T.tr[:, 4 * (b % 2) + t:1024:8], T.gb[:, c:c + 128]).then_inc(S.tt, 1)

    for k, ps, ranks in (("0", T.p0, far[0]), ("n", T.p1, chips[me]), ("1", T.p0, far[1])):
        for b in range(4):
            store(queue(b), k, ps, ranks, b)
        if k == "n":
            v.wait_ge(S.ssg, 8)
            v.tensor_copy(T.so[:], T.sg[:]).then_inc(S.sso, 1)
    store(v, "2", T.p1, far[2], 0)
    pick(v, 0, 0, 512, S.gg0)
    store(s, "2", T.p1, far[2], 2)
    store(s, "2", T.p1, far[2], 3)
    pick(s, 3, 0, 512, S.gg3)
    pick(v, 2, 0, 512, S.gg2)
    store(s, "2", T.p1, far[2], 1)
    pick(s, 1, 0, 512, S.gg1)
    turn(2, range(4), S.gg2)
    turn(3, range(4), S.gg3)
    v.wait_ge(S.sa, 16)
    v.quantize_mx(T.qm[:], T.xm[:], T.at[:]).then_inc(S.sqm, 1)
    sy.wait_ge(S.tt, 8)
    for a in range(4):
        c = 1024 + 256 * a
        sy.dma_start(out=T.ht[:, c:c + 256], in_=T.tr[32 * a:32 * a + 32, :]).then_inc(S["hd%d" % (2 + a // 2)], 16)

    for sem in (S.sdn, S.gg0):
        te.wait_ge(sem, 1)
    for t in range(4):
        te.transpose(T.p0[:, t:512:4], T.gf[:, t:512:4], T.idn[:]).then_inc(S.tp, 1)
    s.wait_ge(S.tp, 4)
    copy(s, T.ht[:, 0:512], T.p0[:, 0:512], S.hd0, 32)
    for sem in (S.gg1, S.c11, S.c12, S.c13, S.c22):
        te.wait_ge(sem, 1)
    for t in range(4):
        bank = T.p0[:, 512 * t + 512:512 * t + 640] if t < 3 else T.p1[:, 1024:1152]
        te.transpose(bank, T.gf[:, 512 + t:1024:4], T.idn[:]).then_inc(S["u%d" % t], 1)
        s.wait_ge(S["u%d" % t], 1)
        copy(s, T.ht[:, 512 + t:1024:4], bank, S.hd1, 8)

    parts = [(0, 0, 512, T.p1, 0, s), (2, 0, 512, T.p1, 1536, v), (1, 0, 256, T.p1, 512, s), (1, 256, 256, T.p0, 0, s),
             (3, 0, 256, T.p0, 512, v), (3, 256, 256, T.p0, 1024, s)]
    for b in (0, 2, 1, 3):
        v.wait_ge(S["hd%d" % b], 32)
        v.quantize_mx(T.qh[:, 128 * b:128 * b + 128], T.xh[:, 128 * b:128 * b + 128], T.ht[:, 512 * b:512 * b + 512]).then_inc(S["hq%d" % b], 1)
    te.wait_ge(S.sqm, 1)
    for i, (b, a, n, ps, at, qu) in enumerate(parts):
        te.wait_ge(S["hq%d" % b], 1)
        te.matmul_mx(ps[:, at:at + n], T.qh[:, 128 * b:128 * b + 128], T.xh[:, 128 * b:128 * b + 128],
                     T.qm[:, a:a + n], T.xm[:, a:a + n], True, True).then_inc(S["ym%d" % i], 1)
        qu.wait_ge(S["ym%d" % i], 1)
        copy(qu, T.yt[:, 512 * b + a:512 * b + a + n], ps[:, at:at + n], S["yc%d" % i])

    for what, i in [("h", b) for b in (0, 2, 1, 3)] + [("y", i) for i in range(len(parts))]:
        if what == "h":
            sy.wait_ge(S["hd%d" % i], 32)
            sy.dma_start(out=T.h[:, 512 * i:512 * i + 512], in_=T.ht[:, 512 * i:512 * i + 512]).then_inc(S.sh, 16)
        else:
            b, a, n = parts[i][0:3]
            c = slice(512 * b + a, 512 * b + a + n)
            sy.wait_ge(S["yc%d" % i], 1)
            sy.dma_start(out=T.y[:, c], in_=T.yt[:, c]).then_inc(S.sy, 16)
    sy.wait_ge(S.sh, 64)
    sy.wait_ge(S.sy, 16 * len(parts))
